import numpy as np
import ml_dtypes


def mxq(x, axis, fmt="e4m3"):
    dtype, down = {"e4m3": (ml_dtypes.float8_e4m3fn, 7), "e5m2": (ml_dtypes.float8_e5m2, 14)}[fmt]
    v = np.moveaxis(np.asarray(x, np.float32).astype(ml_dtypes.bfloat16).astype(np.float64), axis, -1)
    blocks = v.reshape(v.shape[:-1] + (-1, 32))
    amax = np.abs(blocks).max(-1, keepdims=True)
    byte = np.maximum(np.where(amax > 0, np.frexp(amax)[1] - 1 + 127, 0) - down, 1)
    scale = np.exp2(byte - 127.0)
    codes = (blocks / scale).astype(np.float32).astype(dtype).astype(np.float64)
    return np.moveaxis((codes * scale).reshape(v.shape), -1, axis)


WIDE = False


def mx_kscale(k):
    if not WIDE:
        return np.ones(k)
    levels = np.array([10, -10, 5, -5, 0])
    if k % 512:
        return np.exp2(np.random.permutation(np.resize(levels, k // 32))).repeat(32)
    a = np.empty((k // 512, 16))
    for p in range(k // 512):
        a[p, :8] = np.random.permutation(np.resize(levels, 8))
        for g in range(8):
            far = levels[np.abs(levels - a[p, g]) >= 10]
            a[p, g + 8] = far[np.random.randint(len(far))]
    return np.exp2(a.ravel()).repeat(32)


def f64(x):
    return np.asarray(x).astype(np.float64)


def striped(idx):
    return np.tile(idx.reshape(-1, 16).T, (8, 1)).astype(np.uint16)


def unstriped(offs):
    return offs[:16].T.reshape(-1).astype(np.int64)


def striped8(idx):
    return np.concatenate([x.reshape(-1, 16).T for x in idx]).astype(np.uint16)


def runs(offs, k):
    lists = np.stack([offs[16 * r : 16 * r + 16].T.reshape(-1) for r in range(8)]).astype(np.int64)
    return lists[np.arange(k) % 512 // 64]


def pack_weight(w):
    k, n = w.shape
    w = f64(np.asarray(w, np.float32).astype(ml_dtypes.bfloat16)).reshape(k // 32, 32, n)
    amax = np.abs(w).max(1)
    byte = np.clip(np.where(amax > 0, np.frexp(amax)[1] - 1 + 127 - 7, 1), 1, 254)
    scaled = (w * np.exp2(127.0 - byte)[:, None, :]).reshape(k, n).astype(np.float32)
    words = np.ascontiguousarray(scaled.reshape(k // 512, 128, 4, n).transpose(0, 1, 3, 2)).astype(ml_dtypes.float8_e4m3fn).view(np.uint8)
    return words, np.ascontiguousarray(byte.astype(np.uint8).reshape(k // 512, 16, n))


def unpack_weight(words, scales):
    g, p, n, _ = words.shape
    vals = np.ascontiguousarray(words).view(ml_dtypes.float8_e4m3fn).astype(np.float64) * np.repeat(np.exp2(scales.astype(np.float64) - 127.0), 8, axis=1)[..., None]
    return vals.transpose(0, 1, 3, 2).reshape(g * 512, n)


def sigmoid(v):
    return 1.0 / (1.0 + np.exp(-np.maximum(v, -700.0)))


K, T, S, H, C, W = 512, 2048, 512, 512, 512, 256


def setup_inputs():
    n = np.random.standard_normal
    s = mx_kscale(K)[:, None]
    packed_xT = pack_weight(n((K, T)) * s)
    return {
        "x_words": packed_xT[0],
        "x_scales": packed_xT[1],
        "w1": (n((K, H)) / np.sqrt(K) / s).astype(np.float32),
        "gs": (np.random.uniform(0.5, 1.5, (K, 1)) / s).astype(np.float32),
        "offs": striped(np.random.permutation(T)[:S]),
        "n1": striped8(np.stack([np.random.permutation(S) for _ in range(8)])),
        "ca": striped(np.random.permutation(T)[:C]),
        "hc": striped8(np.random.randint(0, T, (8, C))),
        "n2": striped(np.random.permutation(S)[:W]),
        "n3": striped(np.random.permutation(S)[:W]),
    }


def reference(x_words, x_scales, w1, gs, offs, n1, ca, hc, n2, n3):
    x_hc = unpack_weight(x_words, x_scales)[np.arange(K)[:, None], runs(hc, K)]
    xq = unpack_weight(x_words, x_scales)[:, unstriped(offs)]
    y = mxq(f64(w1), 0, "e4m3").T @ xq
    z = f64(gs) * (y * (sigmoid(y[np.arange(H)[:, None], runs(n1, H)])))
    zq = mxq(z, 0, "e4m3")
    b = 0.0625 * (x_hc.T @ zq)
    x_ca = unpack_weight(x_words, x_scales)[:, unstriped(ca)]
    a = 0.0625 * (x_ca.T @ zq)
    ra = b[:, unstriped(n3)] - (0.5 * a[:, unstriped(n2)])
    out = a.copy()
    out[:, unstriped(n2)] = ra
    return out

@@ -1,0 +1,214 @@
+from contextlib import ExitStack
+
+import concourse.mybir as mybir
+
+K, T, S, H, C, W = 512, 2048, 512, 512, 512, 256
+FLOPS = 3 * 2 * 512 * 512 * 512
+
+F32 = mybir.dt.float32
+BF16 = mybir.dt.bfloat16
+I32 = mybir.dt.int32
+U32 = mybir.dt.uint32
+U16 = mybir.dt.uint16
+U8 = mybir.dt.uint8
+FP8X4 = mybir.dt.float8_e4m3fn_x4
+ACT = mybir.ActivationFunctionType
+ALU = mybir.AluOpType
+
+P = 128
+PACK = 4
+BLOCKS = C // P
+HALF = 256
+Z_CHUNKS = ((0, 256), (256, 256))
+SCALAR_PLANES = (0,)
+GATE_SLOTS = 4
+SCALAR_CAST = 96
+
+
+def tile_picked_cdhputbgate_none_p_kernel(
+    tc, x_words, x_scales, w1, gs, offs, n1, ca, hc, n2, n3, out
+):
+    nc = tc.nc
+    with ExitStack() as ctx:
+        keep = ctx.enter_context(tc.tile_pool(name="keep", bufs=1))
+        psum = ctx.enter_context(tc.psum_pool(name="psum", bufs=1))
+
+        def load_list(src, name):
+            tile = keep.tile(list(src.shape), U16, name=name)
+            nc.sync.dma_start(tile[:], src)
+            return tile
+
+        def bank(name, number):
+            return psum.tile([P, S], F32, name=name, tag="bank%d" % number)
+
+        def entries(offsets, first, count):
+            return offsets[:, first // 16 : (first + count) // 16]
+
+        scale_table = keep.tile([P, T], U8, name="scale_table", align_bytes=64)
+        nc.vector.memset(scale_table[:].bitcast(I32), 0)
+        run_table = keep.tile([P, T], U8, name="run_table", align_bytes=64)
+        nc.vector.memset(run_table[:].bitcast(I32), 0)
+        hc_scales = keep.tile([P, C], U8, name="hc_scales", align_bytes=64)
+        nc.vector.memset(hc_scales[:].bitcast(I32), 0)
+
+        offs_t = load_list(offs, "offs_t")
+        ca_t = load_list(ca, "ca_t")
+        hc_t = load_list(hc, "hc_t")
+        scale_rows = x_scales[0].bitcast(I32)
+        for q in range(4):
+            nc.sync.dma_start(scale_table[32 * q : 32 * q + 4, :].bitcast(I32), scale_rows[4 * q : 4 * q + 4, :])
+        word_table = keep.tile([P, T], U32, name="word_table", align_bytes=64)
+        nc.sync.dma_start(word_table[:].bitcast(I32), x_words[0].rearrange("p n t -> p (n t)").bitcast(I32))
+        nc.sync.dma_start(run_table[0:P:8, :].bitcast(I32), scale_rows)
+        w_view = w1.rearrange("(p j) c -> p j c", j=PACK)
+        w_raw = []
+        for h in range(2):
+            raw = keep.tile([P, PACK, HALF], F32, name="w_raw%d" % h)
+            nc.sync.dma_start(raw[:], w_view[:, :, h * HALF : (h + 1) * HALF])
+            w_raw.append(raw)
+        n1_t = load_list(n1, "n1_t")
+        gs_t = keep.tile([P, PACK], F32, name="gs_t")
+        nc.sync.dma_start(gs_t[:], gs.rearrange("(p t) o -> p (t o)", t=PACK))
+        n2_t = load_list(n2, "n2_t")
+        n3_t = load_list(n3, "n3_t")
+
+        def gather(picked, table, offsets):
+            nc.vector.tensor_copy(picked, table[:].indirect(offsets))
+
+        tok_scales = keep.tile([P, S], U8, name="tok_scales", align_bytes=64)
+        gather(tok_scales[:], scale_table, offs_t[:])
+        early_scales = keep.tile([P, HALF], U8, name="early_scales", align_bytes=64)
+        gather(early_scales[:], scale_table, entries(ca_t, 0, HALF))
+        tok_words = keep.tile([P, S], U32, name="tok_words", align_bytes=64)
+        gather(tok_words[:], word_table, offs_t[:])
+
+        hc_spread = keep.tile([P, C], U8, name="hc_spread", align_bytes=64)
+        gather(hc_spread[:], run_table, hc_t[:])
+        for i in range(4):
+            nc.sync.dma_start(hc_scales[i:P:32, :].bitcast(I32), hc_spread[8 * i : P : 32, :].bitcast(I32))
+
+        w_bf = keep.tile([P, PACK, P, PACK], BF16, name="w_bf", tag="w_bf", align_bytes=64)
+
+        def cast(engine_copy, h, lo, hi):
+            src = w_raw[h][:, :, lo:hi].rearrange("p j (m t) -> p m t j", t=PACK)
+            dst = w_bf[:, :, (h * HALF + lo) // PACK : (h * HALF + hi) // PACK, :].rearrange("p t m j -> p m t j")
+            engine_copy(dst, src)
+
+        cast(nc.scalar.copy, 0, 0, HALF)
+        cast(nc.scalar.copy, 1, 0, SCALAR_CAST)
+        cast(nc.vector.tensor_copy, 1, SCALAR_CAST, HALF)
+
+        y_banks, windows = [], []
+        for t in range(PACK):
+            w_words = keep.tile([P, P], U32, name="w_words%d" % t, align_bytes=64)
+            w_scales = keep.tile([P, P], U8, name="w_scales%d" % t, align_bytes=64)
+            nc.vector.quantize_mx(
+                out=w_words[:].bitcast(FP8X4), scales=w_scales[:], in_=w_bf[:, t].rearrange("p m j -> p (m j)")
+            )
+            y_bank = bank("y%d" % t, t)
+            nc.tensor.matmul_mx(
+                out=y_bank[:], lhsT=w_words[:].bitcast(FP8X4), lhsT_scale=w_scales[:],
+                rhs=tok_words[:].bitcast(FP8X4), rhs_scale=tok_scales[:], start=True, stop=True,
+            )
+            y_banks.append(y_bank)
+
+        early_words = keep.tile([P, 2, HALF], U32, name="early_words", tag="w_bf", align_bytes=64)
+        gather(early_words[:, 0, :], word_table, entries(ca_t, 0, HALF))
+        gather(early_words[:, 1, :], word_table, entries(hc_t, 0, HALF))
+
+        for t in range(PACK):
+            window = keep.tile([P, S], F32, name="window%d" % t)
+            if t in SCALAR_PLANES:
+                nc.scalar.activation(window[:], y_banks[t][:], ACT.Sigmoid)
+            else:
+                nc.vector.tensor_copy(window[:], y_banks[t][:])
+            windows.append(window)
+
+        gates = keep.tile([P, GATE_SLOTS * HALF], F32, name="gates")
+        z_words = keep.tile([P, S], U32, name="z_words", align_bytes=64)
+        z_scales = keep.tile([P, S], U8, name="z_scales", align_bytes=64)
+        a_banks = [bank("a0", 4), bank("a1", 6)]
+        b_banks = [bank("b0", 5), bank("b1", 7)]
+        a_rows = [keep.tile([P, S], F32, name="a_row%d" % r) for r in range(BLOCKS)]
+        b_rows = [keep.tile([P, S], F32, name="b_row%d" % r, tag="b_row%d" % r, align_bytes=64) for r in range(BLOCKS)]
+
+        def product(dst, words, scales, cols):
+            nc.tensor.matmul_mx(
+                out=dst[:, cols], lhsT=words.bitcast(FP8X4), lhsT_scale=scales,
+                rhs=z_words[:, cols].bitcast(FP8X4), rhs_scale=z_scales[:, cols], start=True, stop=True,
+            )
+
+        def leave(on_scalar, dst, src):
+            if on_scalar:
+                nc.scalar.activation(dst, src, ACT.Copy, scale=0.0625)
+            else:
+                nc.vector.tensor_scalar(dst, src, 0.0625, None, ALU.mult)
+
+        for n, (c0, cw) in enumerate(Z_CHUNKS):
+            cols = slice(c0, c0 + cw)
+            z_planes = keep.tile([P, PACK, cw], BF16, name="z_planes%d" % n)
+            for t in range(PACK):
+                slot = (n * PACK + t) % GATE_SLOTS
+                gate = gates[:, slot * HALF : slot * HALF + cw]
+                looked_up = windows[t][:].indirect(entries(n1_t, c0, cw))
+                nc.scalar.activation(gate, looked_up, ACT.Copy if t in SCALAR_PLANES else ACT.Sigmoid)
+                y_src = y_banks[t] if t in SCALAR_PLANES else windows[t]
+                nc.vector.scalar_tensor_tensor(
+                    z_planes[:, t, :], y_src[:, cols], gs_t[:, t : t + 1], gate, ALU.mult, ALU.mult
+                )
+            z_bf = keep.tile([P, cw, PACK], BF16, name="z_bf%d" % n, align_bytes=64)
+            nc.vector.tensor_copy(
+                z_bf[:].rearrange("p (c i) t -> p c t i", i=4), z_planes[:].rearrange("p t (c i) -> p c t i", i=4)
+            )
+            nc.vector.quantize_mx(
+                out=z_words[:, cols].bitcast(FP8X4), scales=z_scales[:, cols], in_=z_bf[:].rearrange("p c t -> p (c t)")
+            )
+            last = n == len(Z_CHUNKS) - 1
+            for r in range(2):
+                rows = slice(r * P, (r + 1) * P)
+                product(a_banks[r], early_words[:, 0, rows], early_scales[:, rows], cols)
+                product(b_banks[r], early_words[:, 1, rows], hc_scales[:, rows], cols)
+            for r in range(2):
+                leave(not last or r == 0, a_rows[r][:, cols], a_banks[r][:, cols])
+                leave(not last, b_rows[r][:, cols], b_banks[r][:, cols])
+
+        halves = [keep.tile([P, W], F32, name="half_a%d" % r, tag="half_a%d" % r, align_bytes=64) for r in range(BLOCKS)]
+        ras = [keep.tile([P, W], F32, name="ra%d" % r) for r in range(BLOCKS)]
+
+        def fetch_a(r):
+            nc.scalar.activation(halves[r][:], a_rows[r][:].indirect(n2_t[:]), ACT.Copy, scale=0.5)
+
+        def combine(r):
+            nc.vector.tensor_tensor(ras[r][:], b_rows[r][:].indirect(n3_t[:]), halves[r][:], ALU.subtract)
+
+        def put_back(r):
+            nc.scalar.activation(a_rows[r][:].indirect(n2_t[:]), ras[r][:], ACT.Copy)
+            nc.sync.dma_start(out[r * P : (r + 1) * P, :], a_rows[r][:])
+
+        for r in range(2):
+            fetch_a(r)
+            combine(r)
+        late_ca = keep.tile([P, HALF], U32, name="late_ca", tag="b_row0", align_bytes=64)
+        gather(late_ca[:], word_table, entries(ca_t, HALF, HALF))
+        late_scales = keep.tile([P, HALF], U8, name="late_scales", tag="half_a0", align_bytes=64)
+        gather(late_scales[:], scale_table, entries(ca_t, HALF, HALF))
+        late_hc = keep.tile([P, HALF], U32, name="late_hc", tag="b_row1", align_bytes=64)
+        gather(late_hc[:], word_table, entries(hc_t, HALF, HALF))
+        put_back(0)
+        put_back(1)
+        whole = slice(0, S)
+        for r in range(2, BLOCKS):
+            rows = slice(r * P, (r + 1) * P)
+            local = slice((r - 2) * P, (r - 1) * P)
+            a_bank = bank("a%d" % r, 2 * (r - 2))
+            product(a_bank, late_ca[:, local], late_scales[:, local], whole)
+            leave(False, a_rows[r][:], a_bank[:])
+            fetch_a(r)
+        for r in range(2, BLOCKS):
+            rows = slice(r * P, (r + 1) * P)
+            local = slice((r - 2) * P, (r - 1) * P)
+            b_bank = bank("b%d" % r, 2 * (r - 2) + 1)
+            product(b_bank, late_hc[:, local], hc_scales[:, rows], whole)
+            leave(False, b_rows[r][:], b_bank[:])
+            combine(r)
+            put_back(r)

@@ -51,6 +51,10 @@ def tile_picked_cdhputbgate_none_p_kernel(
         hc_scales = keep.tile([P, C], U8, name="hc_scales", align_bytes=64)
         nc.vector.memset(hc_scales[:].bitcast(I32), 0)
 
+        warm = keep.tile([P, 2], F32, name="warm")
+        nc.gpsimd.memset(warm[:, 0:1], 0.0)
+        nc.scalar.activation(warm[:, 1:2], warm[:, 0:1], ACT.Sigmoid)
+
         offs_t = load_list(offs, "offs_t")
         ca_t = load_list(ca, "ca_t")
         hc_t = load_list(hc, "hc_t")

@@ -20,7 +20,6 @@ PACK = 4
 BLOCKS = C // P
 HALF = 256
 Z_CHUNKS = ((0, 256), (256, 256))
-SCALAR_PLANES = (0,)
 GATE_SLOTS = 4
 SCALAR_CAST = 96
 
@@ -45,15 +44,12 @@ def tile_picked_cdhputbgate_none_p_kernel(
             return offsets[:, first // 16 : (first + count) // 16]
 
         scale_table = keep.tile([P, T], U8, name="scale_table", align_bytes=64)
-        nc.vector.memset(scale_table[:].bitcast(I32), 0)
+        nc.vector.memset(scale_table[:, : T // 2].bitcast(I32), 0)
+        nc.gpsimd.memset(scale_table[:, T // 2 :].bitcast(I32), 0)
         run_table = keep.tile([P, T], U8, name="run_table", align_bytes=64)
-        nc.vector.memset(run_table[:].bitcast(I32), 0)
+        nc.gpsimd.memset(run_table[:].bitcast(I32), 0)
         hc_scales = keep.tile([P, C], U8, name="hc_scales", align_bytes=64)
-        nc.vector.memset(hc_scales[:].bitcast(I32), 0)
-
-        warm = keep.tile([P, 2], F32, name="warm")
-        nc.gpsimd.memset(warm[:, 0:1], 0.0)
-        nc.scalar.activation(warm[:, 1:2], warm[:, 0:1], ACT.Sigmoid)
+        nc.gpsimd.memset(hc_scales[:].bitcast(I32), 0)
 
         offs_t = load_list(offs, "offs_t")
         ca_t = load_list(ca, "ca_t")
@@ -81,8 +77,8 @@ def tile_picked_cdhputbgate_none_p_kernel(
 
         tok_scales = keep.tile([P, S], U8, name="tok_scales", align_bytes=64)
         gather(tok_scales[:], scale_table, offs_t[:])
-        early_scales = keep.tile([P, HALF], U8, name="early_scales", align_bytes=64)
-        gather(early_scales[:], scale_table, entries(ca_t, 0, HALF))
+        ca_scales = keep.tile([P, C], U8, name="ca_scales", align_bytes=64)
+        gather(ca_scales[:], scale_table, ca_t[:])
         tok_words = keep.tile([P, S], U32, name="tok_words", align_bytes=64)
         gather(tok_words[:], word_table, offs_t[:])
 
@@ -102,31 +98,40 @@ def tile_picked_cdhputbgate_none_p_kernel(
         cast(nc.scalar.copy, 1, 0, SCALAR_CAST)
         cast(nc.vector.tensor_copy, 1, SCALAR_CAST, HALF)
 
-        y_banks, windows = [], []
-        for t in range(PACK):
-            w_words = keep.tile([P, P], U32, name="w_words%d" % t, align_bytes=64)
-            w_scales = keep.tile([P, P], U8, name="w_scales%d" % t, align_bytes=64)
+        w_words = keep.tile([P, PACK * P], U32, name="w_words", align_bytes=64)
+        w_scales = keep.tile([P, PACK * P], U8, name="w_scales", align_bytes=64)
+        for first, end in ((0, 1), (1, PACK)):
             nc.vector.quantize_mx(
-                out=w_words[:].bitcast(FP8X4), scales=w_scales[:], in_=w_bf[:, t].rearrange("p m j -> p (m j)")
+                out=w_words[:, first * P : end * P].bitcast(FP8X4),
+                scales=w_scales[:, first * P : end * P],
+                in_=w_bf[:, first:end].rearrange("p t m j -> p (t m j)"),
             )
-            y_bank = bank("y%d" % t, t)
+
+        def project(dst, t, cols):
             nc.tensor.matmul_mx(
-                out=y_bank[:], lhsT=w_words[:].bitcast(FP8X4), lhsT_scale=w_scales[:],
-                rhs=tok_words[:].bitcast(FP8X4), rhs_scale=tok_scales[:], start=True, stop=True,
+                out=dst[:, cols], lhsT=w_words[:, t * P : (t + 1) * P].bitcast(FP8X4),
+                lhsT_scale=w_scales[:, t * P : (t + 1) * P],
+                rhs=tok_words[:, cols].bitcast(FP8X4), rhs_scale=tok_scales[:, cols], start=True, stop=True,
             )
-            y_banks.append(y_bank)
+
+        windows = [keep.tile([P, S], F32, name="window%d" % t) for t in range(PACK)]
+        y0_banks = [bank("y0_0", 0), bank("y0_1", 7)]
+        for h in range(2):
+            cols = slice(h * HALF, (h + 1) * HALF)
+            project(y0_banks[h], 0, cols)
+            nc.scalar.activation(windows[0][:, cols], y0_banks[h][:, cols], ACT.Sigmoid)
+        y_banks = [None]
+        for t in range(1, PACK):
+            y_banks.append(bank("y%d" % t, t))
+            project(y_banks[t], t, slice(0, S))
 
         early_words = keep.tile([P, 2, HALF], U32, name="early_words", tag="w_bf", align_bytes=64)
         gather(early_words[:, 0, :], word_table, entries(ca_t, 0, HALF))
         gather(early_words[:, 1, :], word_table, entries(hc_t, 0, HALF))
 
-        for t in range(PACK):
-            window = keep.tile([P, S], F32, name="window%d" % t)
-            if t in SCALAR_PLANES:
-                nc.scalar.activation(window[:], y_banks[t][:], ACT.Sigmoid)
-            else:
-                nc.vector.tensor_copy(window[:], y_banks[t][:])
-            windows.append(window)
+        nc.scalar.copy(windows[1][:], y_banks[1][:])
+        for t in range(2, PACK):
+            nc.vector.tensor_copy(windows[t][:], y_banks[t][:])
 
         gates = keep.tile([P, GATE_SLOTS * HALF], F32, name="gates")
         z_words = keep.tile([P, S], U32, name="z_words", align_bytes=64)
@@ -155,12 +160,12 @@ def tile_picked_cdhputbgate_none_p_kernel(
                 slot = (n * PACK + t) % GATE_SLOTS
                 gate = gates[:, slot * HALF : slot * HALF + cw]
                 looked_up = windows[t][:].indirect(entries(n1_t, c0, cw))
-                nc.scalar.activation(gate, looked_up, ACT.Copy if t in SCALAR_PLANES else ACT.Sigmoid)
-                y_src = y_banks[t] if t in SCALAR_PLANES else windows[t]
+                nc.scalar.activation(gate, looked_up, ACT.Copy if t == 0 else ACT.Sigmoid)
+                y_src = y0_banks[n] if t == 0 else windows[t]
                 nc.vector.scalar_tensor_tensor(
                     z_planes[:, t, :], y_src[:, cols], gs_t[:, t : t + 1], gate, ALU.mult, ALU.mult
                 )
-            z_bf = keep.tile([P, cw, PACK], BF16, name="z_bf%d" % n, align_bytes=64)
+            z_bf = keep.tile([P, cw, PACK], BF16, name="z_bf%d" % n, tag="z_bf%d" % n, align_bytes=64)
             nc.vector.tensor_copy(
                 z_bf[:].rearrange("p (c i) t -> p c t i", i=4), z_planes[:].rearrange("p t (c i) -> p c t i", i=4)
             )
@@ -170,13 +175,13 @@ def tile_picked_cdhputbgate_none_p_kernel(
             last = n == len(Z_CHUNKS) - 1
             for r in range(2):
                 rows = slice(r * P, (r + 1) * P)
-                product(a_banks[r], early_words[:, 0, rows], early_scales[:, rows], cols)
+                product(a_banks[r], early_words[:, 0, rows], ca_scales[:, rows], cols)
                 product(b_banks[r], early_words[:, 1, rows], hc_scales[:, rows], cols)
             for r in range(2):
                 leave(not last or r == 0, a_rows[r][:, cols], a_banks[r][:, cols])
                 leave(not last, b_rows[r][:, cols], b_banks[r][:, cols])
 
-        halves = [keep.tile([P, W], F32, name="half_a%d" % r, tag="half_a%d" % r, align_bytes=64) for r in range(BLOCKS)]
+        halves = [keep.tile([P, W], F32, name="half_a%d" % r) for r in range(BLOCKS)]
         ras = [keep.tile([P, W], F32, name="ra%d" % r) for r in range(BLOCKS)]
 
         def fetch_a(r):
@@ -192,11 +197,9 @@ def tile_picked_cdhputbgate_none_p_kernel(
         for r in range(2):
             fetch_a(r)
             combine(r)
-        late_ca = keep.tile([P, HALF], U32, name="late_ca", tag="b_row0", align_bytes=64)
+        late_ca = keep.tile([P, HALF], U32, name="late_ca", tag="z_bf1", align_bytes=64)
         gather(late_ca[:], word_table, entries(ca_t, HALF, HALF))
-        late_scales = keep.tile([P, HALF], U8, name="late_scales", tag="half_a0", align_bytes=64)
-        gather(late_scales[:], scale_table, entries(ca_t, HALF, HALF))
-        late_hc = keep.tile([P, HALF], U32, name="late_hc", tag="b_row1", align_bytes=64)
+        late_hc = keep.tile([P, HALF], U32, name="late_hc", tag="b_row0", align_bytes=64)
         gather(late_hc[:], word_table, entries(hc_t, HALF, HALF))
         put_back(0)
         put_back(1)
@@ -205,7 +208,7 @@ def tile_picked_cdhputbgate_none_p_kernel(
             rows = slice(r * P, (r + 1) * P)
             local = slice((r - 2) * P, (r - 1) * P)
             a_bank = bank("a%d" % r, 2 * (r - 2))
-            product(a_bank, late_ca[:, local], late_scales[:, local], whole)
+            product(a_bank, late_ca[:, local], ca_scales[:, rows], whole)
             leave(False, a_rows[r][:], a_bank[:])
             fetch_a(r)
         for r in range(2, BLOCKS):

@@ -51,6 +51,10 @@ def tile_picked_cdhputbgate_none_p_kernel(
         hc_scales = keep.tile([P, C], U8, name="hc_scales", align_bytes=64)
         nc.gpsimd.memset(hc_scales[:].bitcast(I32), 0)
 
+        warm = keep.tile([P, 2], F32, name="warm")
+        nc.gpsimd.memset(warm[:, 0:1], 0.0)
+        nc.scalar.activation(warm[:, 1:2], warm[:, 0:1], ACT.Sigmoid)
+
         offs_t = load_list(offs, "offs_t")
         ca_t = load_list(ca, "ca_t")
         hc_t = load_list(hc, "hc_t")

from contextlib import ExitStack

import concourse.mybir as mybir

K, T, S, H, C, W = 512, 2048, 512, 512, 512, 256
FLOPS = 3 * 2 * 512 * 512 * 512

F32 = mybir.dt.float32
BF16 = mybir.dt.bfloat16
I32 = mybir.dt.int32
U32 = mybir.dt.uint32
U16 = mybir.dt.uint16
U8 = mybir.dt.uint8
FP8X4 = mybir.dt.float8_e4m3fn_x4
ACT = mybir.ActivationFunctionType
ALU = mybir.AluOpType

P = 128
PACK = 4
BLOCKS = C // P
HALF = 256
Z_CHUNKS = ((0, 256), (256, 256))
GATE_SLOTS = 4
SCALAR_CAST = 96


def tile_picked_cdhputbgate_none_p_kernel(
    tc, x_words, x_scales, w1, gs, offs, n1, ca, hc, n2, n3, out
):
    nc = tc.nc
    with ExitStack() as ctx:
        keep = ctx.enter_context(tc.tile_pool(name="keep", bufs=1))
        psum = ctx.enter_context(tc.psum_pool(name="psum", bufs=1))

        def load_list(src, name):
            tile = keep.tile(list(src.shape), U16, name=name)
            nc.sync.dma_start(tile[:], src)
            return tile

        def bank(name, number):
            return psum.tile([P, S], F32, name=name, tag="bank%d" % number)

        def entries(offsets, first, count):
            return offsets[:, first // 16 : (first + count) // 16]

        scale_table = keep.tile([P, T], U8, name="scale_table", align_bytes=64)
        nc.vector.memset(scale_table[:, : T // 2].bitcast(I32), 0)
        nc.gpsimd.memset(scale_table[:, T // 2 :].bitcast(I32), 0)
        run_table = keep.tile([P, T], U8, name="run_table", align_bytes=64)
        nc.gpsimd.memset(run_table[:].bitcast(I32), 0)
        hc_scales = keep.tile([P, C], U8, name="hc_scales", align_bytes=64)
        nc.gpsimd.memset(hc_scales[:].bitcast(I32), 0)

        warm = keep.tile([P, 2], F32, name="warm")
        nc.gpsimd.memset(warm[:, 0:1], 0.0)
        nc.scalar.activation(warm[:, 1:2], warm[:, 0:1], ACT.Sigmoid)

        offs_t = load_list(offs, "offs_t")
        ca_t = load_list(ca, "ca_t")
        hc_t = load_list(hc, "hc_t")
        scale_rows = x_scales[0].bitcast(I32)
        for q in range(4):
            nc.sync.dma_start(scale_table[32 * q : 32 * q + 4, :].bitcast(I32), scale_rows[4 * q : 4 * q + 4, :])
        word_table = keep.tile([P, T], U32, name="word_table", align_bytes=64)
        nc.sync.dma_start(word_table[:].bitcast(I32), x_words[0].rearrange("p n t -> p (n t)").bitcast(I32))
        nc.sync.dma_start(run_table[0:P:8, :].bitcast(I32), scale_rows)
        w_view = w1.rearrange("(p j) c -> p j c", j=PACK)
        w_raw = []
        for h in range(2):
            raw = keep.tile([P, PACK, HALF], F32, name="w_raw%d" % h)
            nc.sync.dma_start(raw[:], w_view[:, :, h * HALF : (h + 1) * HALF])
            w_raw.append(raw)
        n1_t = load_list(n1, "n1_t")
        gs_t = keep.tile([P, PACK], F32, name="gs_t")
        nc.sync.dma_start(gs_t[:], gs.rearrange("(p t) o -> p (t o)", t=PACK))
        n2_t = load_list(n2, "n2_t")
        n3_t = load_list(n3, "n3_t")

        def gather(picked, table, offsets):
            nc.vector.tensor_copy(picked, table[:].indirect(offsets))

        tok_scales = keep.tile([P, S], U8, name="tok_scales", align_bytes=64)
        gather(tok_scales[:], scale_table, offs_t[:])
        ca_scales = keep.tile([P, C], U8, name="ca_scales", align_bytes=64)
        gather(ca_scales[:], scale_table, ca_t[:])
        tok_words = keep.tile([P, S], U32, name="tok_words", align_bytes=64)
        gather(tok_words[:], word_table, offs_t[:])

        hc_spread = keep.tile([P, C], U8, name="hc_spread", align_bytes=64)
        gather(hc_spread[:], run_table, hc_t[:])
        for i in range(4):
            nc.sync.dma_start(hc_scales[i:P:32, :].bitcast(I32), hc_spread[8 * i : P : 32, :].bitcast(I32))

        w_bf = keep.tile([P, PACK, P, PACK], BF16, name="w_bf", tag="w_bf", align_bytes=64)

        def cast(engine_copy, h, lo, hi):
            src = w_raw[h][:, :, lo:hi].rearrange("p j (m t) -> p m t j", t=PACK)
            dst = w_bf[:, :, (h * HALF + lo) // PACK : (h * HALF + hi) // PACK, :].rearrange("p t m j -> p m t j")
            engine_copy(dst, src)

        cast(nc.scalar.copy, 0, 0, HALF)
        cast(nc.scalar.copy, 1, 0, SCALAR_CAST)
        cast(nc.vector.tensor_copy, 1, SCALAR_CAST, HALF)

        w_words = keep.tile([P, PACK * P], U32, name="w_words", align_bytes=64)
        w_scales = keep.tile([P, PACK * P], U8, name="w_scales", align_bytes=64)
        for first, end in ((0, 1), (1, PACK)):
            nc.vector.quantize_mx(
                out=w_words[:, first * P : end * P].bitcast(FP8X4),
                scales=w_scales[:, first * P : end * P],
                in_=w_bf[:, first:end].rearrange("p t m j -> p (t m j)"),
            )

        def project(dst, t, cols):
            nc.tensor.matmul_mx(
                out=dst[:, cols], lhsT=w_words[:, t * P : (t + 1) * P].bitcast(FP8X4),
                lhsT_scale=w_scales[:, t * P : (t + 1) * P],
                rhs=tok_words[:, cols].bitcast(FP8X4), rhs_scale=tok_scales[:, cols], start=True, stop=True,
            )

        windows = [keep.tile([P, S], F32, name="window%d" % t) for t in range(PACK)]
        y0_banks = [bank("y0_0", 0), bank("y0_1", 7)]
        for h in range(2):
            cols = slice(h * HALF, (h + 1) * HALF)
            project(y0_banks[h], 0, cols)
            nc.scalar.activation(windows[0][:, cols], y0_banks[h][:, cols], ACT.Sigmoid)
        y_banks = [None]
        for t in range(1, PACK):
            y_banks.append(bank("y%d" % t, t))
            project(y_banks[t], t, slice(0, S))

        early_words = keep.tile([P, 2, HALF], U32, name="early_words", tag="w_bf", align_bytes=64)
        gather(early_words[:, 0, :], word_table, entries(ca_t, 0, HALF))
        gather(early_words[:, 1, :], word_table, entries(hc_t, 0, HALF))

        nc.scalar.copy(windows[1][:], y_banks[1][:])
        for t in range(2, PACK):
            nc.vector.tensor_copy(windows[t][:], y_banks[t][:])

        gates = keep.tile([P, GATE_SLOTS * HALF], F32, name="gates")
        z_words = keep.tile([P, S], U32, name="z_words", align_bytes=64)
        z_scales = keep.tile([P, S], U8, name="z_scales", align_bytes=64)
        a_banks = [bank("a0", 4), bank("a1", 6)]
        b_banks = [bank("b0", 5), bank("b1", 7)]
        a_rows = [keep.tile([P, S], F32, name="a_row%d" % r) for r in range(BLOCKS)]
        b_rows = [keep.tile([P, S], F32, name="b_row%d" % r, tag="b_row%d" % r, align_bytes=64) for r in range(BLOCKS)]

        def product(dst, words, scales, cols):
            nc.tensor.matmul_mx(
                out=dst[:, cols], lhsT=words.bitcast(FP8X4), lhsT_scale=scales,
                rhs=z_words[:, cols].bitcast(FP8X4), rhs_scale=z_scales[:, cols], start=True, stop=True,
            )

        def leave(on_scalar, dst, src):
            if on_scalar:
                nc.scalar.activation(dst, src, ACT.Copy, scale=0.0625)
            else:
                nc.vector.tensor_scalar(dst, src, 0.0625, None, ALU.mult)

        for n, (c0, cw) in enumerate(Z_CHUNKS):
            cols = slice(c0, c0 + cw)
            z_planes = keep.tile([P, PACK, cw], BF16, name="z_planes%d" % n)
            for t in range(PACK):
                slot = (n * PACK + t) % GATE_SLOTS
                gate = gates[:, slot * HALF : slot * HALF + cw]
                looked_up = windows[t][:].indirect(entries(n1_t, c0, cw))
                nc.scalar.activation(gate, looked_up, ACT.Copy if t == 0 else ACT.Sigmoid)
                y_src = y0_banks[n] if t == 0 else windows[t]
                nc.vector.scalar_tensor_tensor(
                    z_planes[:, t, :], y_src[:, cols], gs_t[:, t : t + 1], gate, ALU.mult, ALU.mult
                )
            z_bf = keep.tile([P, cw, PACK], BF16, name="z_bf%d" % n, tag="z_bf%d" % n, align_bytes=64)
            nc.vector.tensor_copy(
                z_bf[:].rearrange("p (c i) t -> p c t i", i=4), z_planes[:].rearrange("p t (c i) -> p c t i", i=4)
            )
            nc.vector.quantize_mx(
                out=z_words[:, cols].bitcast(FP8X4), scales=z_scales[:, cols], in_=z_bf[:].rearrange("p c t -> p (c t)")
            )
            last = n == len(Z_CHUNKS) - 1
            for r in range(2):
                rows = slice(r * P, (r + 1) * P)
                product(a_banks[r], early_words[:, 0, rows], ca_scales[:, rows], cols)
                product(b_banks[r], early_words[:, 1, rows], hc_scales[:, rows], cols)
            for r in range(2):
                leave(not last or r == 0, a_rows[r][:, cols], a_banks[r][:, cols])
                leave(not last, b_rows[r][:, cols], b_banks[r][:, cols])

        halves = [keep.tile([P, W], F32, name="half_a%d" % r) for r in range(BLOCKS)]
        ras = [keep.tile([P, W], F32, name="ra%d" % r) for r in range(BLOCKS)]

        def fetch_a(r):
            nc.scalar.activation(halves[r][:], a_rows[r][:].indirect(n2_t[:]), ACT.Copy, scale=0.5)

        def combine(r):
            nc.vector.tensor_tensor(ras[r][:], b_rows[r][:].indirect(n3_t[:]), halves[r][:], ALU.subtract)

        def put_back(r):
            nc.scalar.activation(a_rows[r][:].indirect(n2_t[:]), ras[r][:], ACT.Copy)
            nc.sync.dma_start(out[r * P : (r + 1) * P, :], a_rows[r][:])

        for r in range(2):
            fetch_a(r)
            combine(r)
        late_ca = keep.tile([P, HALF], U32, name="late_ca", tag="z_bf1", align_bytes=64)
        gather(late_ca[:], word_table, entries(ca_t, HALF, HALF))
        late_hc = keep.tile([P, HALF], U32, name="late_hc", tag="b_row0", align_bytes=64)
        gather(late_hc[:], word_table, entries(hc_t, HALF, HALF))
        put_back(0)
        put_back(1)
        whole = slice(0, S)
        for r in range(2, BLOCKS):
            rows = slice(r * P, (r + 1) * P)
            local = slice((r - 2) * P, (r - 1) * P)
            a_bank = bank("a%d" % r, 2 * (r - 2))
            product(a_bank, late_ca[:, local], ca_scales[:, rows], whole)
            leave(False, a_rows[r][:], a_bank[:])
            fetch_a(r)
        for r in range(2, BLOCKS):
            rows = slice(r * P, (r + 1) * P)
            local = slice((r - 2) * P, (r - 1) * P)
            b_bank = bank("b%d" % r, 2 * (r - 2) + 1)
            product(b_bank, late_hc[:, local], hc_scales[:, rows], whole)
            leave(False, b_rows[r][:], b_bank[:])
            combine(r)
            put_back(r)
